import numpy as np
import ml_dtypes


def mxq(x, axis, fmt="e4m3"):
    dtype, down = {"e4m3": (ml_dtypes.float8_e4m3fn, 7), "e5m2": (ml_dtypes.float8_e5m2, 14)}[fmt]
    v = np.moveaxis(np.asarray(x, np.float32).astype(ml_dtypes.bfloat16).astype(np.float64), axis, -1)
    blocks = v.reshape(v.shape[:-1] + (-1, 32))
    amax = np.abs(blocks).max(-1, keepdims=True)
    byte = np.maximum(np.where(amax > 0, np.frexp(amax)[1] - 1 + 127, 0) - down, 1)
    scale = np.exp2(byte - 127.0)
    codes = (blocks / scale).astype(np.float32).astype(dtype).astype(np.float64)
    return np.moveaxis((codes * scale).reshape(v.shape), -1, axis)


WIDE = False


def mx_kscale(k):
    if not WIDE:
        return np.ones(k)
    levels = np.array([10, -10, 5, -5, 0])
    if k % 512:
        return np.exp2(np.random.permutation(np.resize(levels, k // 32))).repeat(32)
    a = np.empty((k // 512, 16))
    for p in range(k // 512):
        a[p, :8] = np.random.permutation(np.resize(levels, 8))
        for g in range(8):
            far = levels[np.abs(levels - a[p, g]) >= 10]
            a[p, g + 8] = far[np.random.randint(len(far))]
    return np.exp2(a.ravel()).repeat(32)


def f64(x):
    return np.asarray(x).astype(np.float64)


E2M1 = np.array([0.0, 0.5, 1.0, 1.5, 2.0, 3.0, 4.0, 6.0, -0.0, -0.5, -1.0, -1.5, -2.0, -3.0, -4.0, -6.0])


def pack_weight(w, fmt):
    k, n = w.shape
    w = f64(np.asarray(w, np.float32).astype(ml_dtypes.bfloat16)).reshape(k // 32, 32, n)
    amax = np.abs(w).max(1)
    if fmt == "e4m3":
        byte = np.frexp(amax)[1] - 1 + 127 - 7
    else:
        mant, ex = np.frexp(amax / 6.0)
        byte = np.where(mant > 0.5, ex, ex - 1) + 127
    byte = np.clip(np.where(amax > 0, byte, 1), 1, 254)
    scaled = (w * np.exp2(127.0 - byte)[:, None, :]).reshape(k, n).astype(np.float32)
    by_word = np.ascontiguousarray(scaled.reshape(k // 512, 128, 4, n).transpose(0, 1, 3, 2))
    if fmt == "e4m3":
        words = by_word.astype(ml_dtypes.float8_e4m3fn).view(np.uint8)
    else:
        c = by_word.astype(ml_dtypes.float4_e2m1fn).view(np.uint8) & 0xF
        words = (c[..., 0::2] | (c[..., 1::2] << 4)).reshape(k // 512, 128, 2 * n)
    return np.ascontiguousarray(words), np.ascontiguousarray(byte.astype(np.uint8).reshape(k // 512, 16, n))


def unpack_weight(words, scales, fmt):
    g, _, n = scales.shape
    words = np.ascontiguousarray(words).reshape(g, 128, n, -1)
    if fmt == "e4m3":
        vals = words.view(ml_dtypes.float8_e4m3fn).astype(np.float64)
    else:
        nib = np.empty((g, 128, n, 4), np.uint8)
        nib[..., 0::2] = words & 0xF
        nib[..., 1::2] = words >> 4
        vals = E2M1[nib]
    vals = vals * np.repeat(np.exp2(scales.astype(np.float64) - 127.0), 8, axis=1)[..., None]
    return vals.transpose(0, 1, 3, 2).reshape(g * 512, n)


def sigmoid(v):
    return 1.0 / (1.0 + np.exp(-v))


def bf(x):
    return np.asarray(x, np.float32).astype(ml_dtypes.bfloat16)


def planes(Y):
    r, m = Y.shape
    b = f64(bf(Y)).reshape(r // 32, 32, m)
    amax = np.abs(b).max(1)
    byte = np.clip(np.where(amax > 0, np.frexp(amax)[1] - 1 + 127 - 7, 1), 1, 254)
    codes = (b * np.exp2(127.0 - byte)[:, None, :]).reshape(r, m).astype(np.float32).astype(ml_dtypes.float8_e4m3fn).view(np.uint8)
    words = codes.reshape(r // 512, 128, 4, m).transpose(0, 1, 3, 2)
    return np.ascontiguousarray(words), np.ascontiguousarray(byte.astype(np.uint8).reshape(r // 512, 16, m))


K, L, T, N = 1024, 1024, 512, 512


def setup_inputs():
    n = np.random.standard_normal
    fk = mx_kscale(K)
    fl = mx_kscale(L)
    xtp = pack_weight(n((K, T)) / fk[:, None], "e2m1")
    wap = pack_weight(n((K, N)) * 1 / np.sqrt(K) * fk[:, None], "e4m3")
    wqp = pack_weight(n((L, N)) * 1 / np.sqrt(L) * fl[:, None], "e2m1")
    return {
        "xt_words": xtp[0],
        "xt_scales": xtp[1],
        "wa_words": wap[0],
        "wa_scales": wap[1],
        "xq": (n((L, T)) / fl[:, None]).astype(np.float32),
        "wq_words": wqp[0],
        "wq_scales": wqp[1],
        "wc": (n((L, N)) * 1 / np.sqrt(L) * fl[:, None]).astype(np.float32),
    }


def reference(xt_words, xt_scales, wa_words, wa_scales, xq, wq_words, wq_scales, wc):
    xtu = unpack_weight(xt_words, xt_scales, "e2m1")
    wau = unpack_weight(wa_words, wa_scales, "e4m3")
    wqu = unpack_weight(wq_words, wq_scales, "e2m1")
    xqq = mxq(f64(xq), 0, "e4m3")
    z = wau.T @ xtu + wqu.T @ xqq
    zp = np.pad(z, ((0, 0), (1, 0)))[:, :T]
    wcq = mxq(f64(wc), 0, "e4m3")
    s = wcq.T @ xqq
    y = z * sigmoid(zp) + 0.5 * s
    words, scales = planes(y)
    return y, words, scales

@@ -1,0 +1,291 @@
+from contextlib import ExitStack
+
+import concourse.mybir as mybir
+
+K, L, T, N = 1024, 1024, 512, 512
+FLOPS = 2 * N * T * (K + 2 * L)
+
+F32 = mybir.dt.float32
+BF16 = mybir.dt.bfloat16
+I32 = mybir.dt.int32
+U32 = mybir.dt.uint32
+U8 = mybir.dt.uint8
+FP8X4 = mybir.dt.float8_e4m3fn_x4
+FP4X4 = mybir.dt.float4_e2m1fn_x4
+ALU = mybir.AluOpType
+ACT = mybir.ActivationFunctionType
+
+P = 128
+PACK = 4
+PASSES = 2
+K_PASS = P * PACK
+CHUNK = 128
+CHUNKS = T // CHUNK
+HALF = T // 2
+PAD = 4
+
+
+def tile_mix_sum_and_its_own_gate_pl_kernel(
+    tc, xt_words, xt_scales, wa_words, wa_scales, xq, wq_words, wq_scales, wc, out_0, out_1, out_2
+):
+    nc = tc.nc
+    with ExitStack() as ctx:
+        sb = ctx.enter_context(tc.tile_pool(name="sb", bufs=1))
+        ps = ctx.enter_context(tc.psum_pool(name="ps", bufs=1))
+        ctx.enter_context(tc.manual_schedule())
+
+        def tile(name, shape, dtype):
+            return sb.tile(shape, dtype, name=name, align_bytes=64)
+
+        wa_raw = tile("wa_raw", [P, PASSES * N], U32)
+        wa_sraw = tile("wa_sraw", [P, PASSES, N], U8)
+        wq_raw = tile("wq_raw", [P, PASSES, 2 * N], U8)
+        wq_sraw = tile("wq_sraw", [P, PASSES, N], U8)
+        xt_w = tile("xt_w", [P, PASSES, 2 * T], U8)
+        xt_s = tile("xt_s", [P, PASSES, T], U8)
+        wa_w = tile("wa_w", [P, PACK, PASSES * P], U32)
+        wa_s = tile("wa_s", [P, PACK, PASSES * P], U8)
+        wq_w = tile("wq_w", [P, PACK, PASSES * 2 * P], U8)
+        wq_s = tile("wq_s", [P, PACK, PASSES * P], U8)
+        pieces = [(z, h) for z in range(PASSES) for h in range(2)]
+        xq_raw = {zh: tile("xq_raw%d%d" % zh, [P, PACK, HALF], F32) for zh in pieces}
+        xq_bf = {zh: tile("xq_bf%d%d" % zh, [P, HALF, PACK], BF16) for zh in pieces}
+        xq_w = {zh: tile("xq_w%d%d" % zh, [P, HALF], U32) for zh in pieces}
+        xq_s = {zh: tile("xq_s%d%d" % zh, [P, HALF], U8) for zh in pieces}
+        wc_raw = {zh: tile("wc_raw%d%d" % zh, [P, PACK, HALF], F32) for zh in pieces}
+        wc_bf = {zh: tile("wc_bf%d%d" % zh, [P, PACK, P // 2, PACK], BF16) for zh in pieces}
+        zr = [(z, r) for z in range(PASSES) for r in range(PACK)]
+        wc_w = {k: tile("wc_w%d%d" % k, [P, P], U32) for k in zr}
+        wc_s = {k: tile("wc_s%d%d" % k, [P, P], U8) for k in zr}
+        zero = tile("zero", [P, PACK, 1], F32)
+        gate = tile("gate", [P, PACK, PAD + T], F32)
+        gated = [tile("gated%d" % c, [P, PACK, CHUNK], F32) for c in range(CHUNKS)]
+        y = [tile("y%d" % c, [P, PACK, CHUNK], F32) for c in range(CHUNKS)]
+        y_bf = [tile("y_bf%d" % c, [P, CHUNK, PACK], BF16) for c in range(CHUNKS)]
+        y_w = tile("y_w", [P, T], U32)
+        y_s = tile("y_s", [P, T], U8)
+        z_ps = [ps.tile([P, PACK, CHUNK], F32, name="z_ps%d" % c) for c in range(CHUNKS)]
+        s_ps = [ps.tile([P, PACK, CHUNK], F32, name="s_ps%d" % c) for c in range(CHUNKS)]
+
+        def clear(engine, plane):
+            engine.memset(plane[:].rearrange("p z n -> p (z n)").bitcast(I32), 0)
+
+        def load_scales(queue, plane, scales):
+            for q in range(4):
+                queue.dma_start(
+                    out=plane[32 * q : 32 * q + 4, :, :].bitcast(I32),
+                    in_=scales[:, 4 * q : 4 * q + 4, :].rearrange("z r n -> r z n").bitcast(I32),
+                )
+
+        def load_rows(raw, src, z, h):
+            rows = src[z * K_PASS : (z + 1) * K_PASS, h * HALF : (h + 1) * HALF]
+            nc.sync.dma_start(out=raw[(z, h)][:], in_=rows.rearrange("(p j) c -> p j c", j=PACK))
+
+        def copy(on_scalar, out, in_):
+            if on_scalar:
+                nc.scalar.copy(out=out, in_=in_)
+            else:
+                nc.vector.tensor_copy(out=out, in_=in_)
+
+        def round_xq(on_scalar, z, h, lo, hi):
+            copy(
+                on_scalar,
+                xq_bf[(z, h)][:, lo:hi, :].rearrange("p (c i) j -> p c j i", i=4),
+                xq_raw[(z, h)][:, :, lo:hi].rearrange("p j (c i) -> p c j i", i=4),
+            )
+
+        def quantise_xq(z, h):
+            nc.vector.quantize_mx(
+                out=xq_w[(z, h)][:].bitcast(FP8X4),
+                scales=xq_s[(z, h)][:],
+                in_=xq_bf[(z, h)][:].rearrange("p c j -> p (c j)"),
+            )
+
+        def round_wc(on_scalar, z, h, lo, hi):
+            copy(
+                on_scalar,
+                wc_bf[(z, h)][:, :, lo:hi, :].rearrange("p r m j -> p m r j"),
+                wc_raw[(z, h)][:, :, PACK * lo : PACK * hi].rearrange("p j (m r) -> p m r j", r=PACK),
+            )
+
+        def quantise_wc(z, h):
+            cols = slice(h * P // 2, (h + 1) * P // 2)
+            for r in range(PACK):
+                nc.vector.quantize_mx(
+                    out=wc_w[(z, r)][:, cols].bitcast(FP8X4),
+                    scales=wc_s[(z, r)][:, cols],
+                    in_=wc_bf[(z, h)][:, r, :, :].rearrange("p m j -> p (m j)"),
+                )
+
+        def multiply_wa(c):
+            for z in range(PASSES):
+                for r in range(PACK):
+                    nc.tensor.matmul_mx(
+                        out=z_ps[c][:, r, :],
+                        lhsT=wa_w[:, r, z * P : (z + 1) * P].bitcast(FP8X4),
+                        lhsT_scale=wa_s[:, r, z * P : (z + 1) * P],
+                        rhs=xt_w[:, z, 2 * c * CHUNK : 2 * (c + 1) * CHUNK].bitcast(FP4X4),
+                        rhs_scale=xt_s[:, z, c * CHUNK : (c + 1) * CHUNK],
+                        start=(z == 0 and r == 0),
+                        stop=False,
+                    )
+
+        def multiply_wq(z, c):
+            h, lo = divmod(c * CHUNK, HALF)
+            for r in range(PACK):
+                nc.tensor.matmul_mx(
+                    out=z_ps[c][:, r, :],
+                    lhsT=wq_w[:, r, 2 * z * P : 2 * (z + 1) * P].bitcast(FP4X4),
+                    lhsT_scale=wq_s[:, r, z * P : (z + 1) * P],
+                    rhs=xq_w[(z, h)][:, lo : lo + CHUNK].bitcast(FP8X4),
+                    rhs_scale=xq_s[(z, h)][:, lo : lo + CHUNK],
+                    start=False,
+                    stop=(z == PASSES - 1 and r == PACK - 1),
+                )
+
+        def multiply_wc(z, c):
+            h, lo = divmod(c * CHUNK, HALF)
+            for r in range(PACK):
+                nc.tensor.matmul_mx(
+                    out=s_ps[c][:, r, :],
+                    lhsT=wc_w[(z, r)][:].bitcast(FP8X4),
+                    lhsT_scale=wc_s[(z, r)][:],
+                    rhs=xq_w[(z, h)][:, lo : lo + CHUNK].bitcast(FP8X4),
+                    rhs_scale=xq_s[(z, h)][:, lo : lo + CHUNK],
+                    start=(z == 0 and r == 0),
+                    stop=(z == PASSES - 1 and r == PACK - 1),
+                )
+
+        def sigmoid(c):
+            lo = PAD + c * CHUNK
+            nc.scalar.activation(out=gate[:, :, lo : lo + CHUNK], in_=z_ps[c][:], func=ACT.Sigmoid)
+
+        def apply_gate(c):
+            lo = PAD - 1 + c * CHUNK
+            nc.vector.tensor_tensor(out=gated[c][:], in0=z_ps[c][:], in1=gate[:, :, lo : lo + CHUNK], op=ALU.mult)
+
+        def add_s(c):
+            nc.vector.scalar_tensor_tensor(
+                out=y[c][:].rearrange("p r t -> p (r t)"),
+                in0=s_ps[c][:].rearrange("p r t -> p (r t)"),
+                scalar=0.5,
+                in1=gated[c][:].rearrange("p r t -> p (r t)"),
+                op0=ALU.mult,
+                op1=ALU.add,
+            )
+            nc.sync.dma_start(
+                out=out_0[:, c * CHUNK : (c + 1) * CHUNK].rearrange("(p r) t -> p r t", r=PACK), in_=y[c][:]
+            )
+
+        def round_y(c):
+            nc.scalar.copy(
+                out=y_bf[c][:].rearrange("p (c i) r -> p c r i", i=4),
+                in_=y[c][:].rearrange("p r (c i) -> p c r i", i=4),
+            )
+
+        def quantise_y(c):
+            cols = slice(c * CHUNK, (c + 1) * CHUNK)
+            nc.vector.quantize_mx(
+                out=y_w[:, cols].bitcast(FP8X4), scales=y_s[:, cols], in_=y_bf[c][:].rearrange("p t r -> p (t r)")
+            )
+
+        def store_words(lo, hi):
+            words = out_1[0].rearrange("p c r -> p (c r)").bitcast(I32)
+            nc.sync.dma_start(out=words[:, lo:hi], in_=y_w[:, lo:hi].bitcast(I32))
+
+        clear(nc.vector, wa_sraw)
+        clear(nc.gpsimd, xt_s)
+        clear(nc.vector, wq_sraw)
+        nc.vector.memset(zero[:], 0.0)
+        nc.scalar.activation(out=gate[:, :, PAD - 1 : PAD], in_=zero[:], func=ACT.Sigmoid)
+        load_scales(nc.gpsimd, xt_s, xt_scales)
+        nc.sync.dma_start(
+            out=wa_raw[:].rearrange("p (z n) -> p z n", z=PASSES).bitcast(I32),
+            in_=wa_words.rearrange("z p n t -> p z (n t)").bitcast(I32),
+        )
+        load_scales(nc.sync, wa_sraw, wa_scales)
+        nc.sync.dma_start(out=xt_w[:].bitcast(I32), in_=xt_words.rearrange("z p b -> p z b").bitcast(I32))
+        nc.sync.dma_start(out=wq_raw[:].bitcast(I32), in_=wq_words.rearrange("z p b -> p z b").bitcast(I32))
+        load_rows(xq_raw, xq, 0, 0)
+        load_scales(nc.sync, wq_sraw, wq_scales)
+        load_rows(xq_raw, xq, 1, 0)
+        load_rows(xq_raw, xq, 0, 1)
+        load_rows(xq_raw, xq, 1, 1)
+        for z, h in pieces:
+            load_rows(wc_raw, wc, z, h)
+
+        nc.vector.tensor_copy(
+            out=wa_w[:].bitcast(I32).rearrange("p r (b i) -> p b r i", i=4),
+            in_=wa_raw[:].bitcast(I32).rearrange("p (b i r) -> p b r i", i=4, r=PACK),
+        )
+
+        def deal_scales(plane, raw):
+            nc.vector.tensor_copy(
+                out=plane[:].rearrange("p r (b i) -> p b r i", i=16),
+                in_=raw[:].rearrange("p z (b i r) -> p (z b) r i", i=16, r=PACK),
+            )
+
+        deal_scales(wa_s, wa_sraw)
+        nc.vector.tensor_copy(
+            out=wq_w[:].rearrange("p r (b i u) -> p b r i u", i=8, u=2),
+            in_=wq_raw[:].rearrange("p z (b i r u) -> p (z b) r i u", i=8, r=PACK, u=2),
+        )
+        deal_scales(wq_s, wq_sraw)
+
+        multiply_wa(0)
+        multiply_wa(1)
+        round_xq(True, 0, 0, 0, HALF)
+        round_xq(True, 1, 0, 0, HALF // 2)
+        round_xq(False, 1, 0, HALF // 2, HALF)
+        quantise_xq(0, 0)
+        quantise_xq(1, 0)
+        multiply_wq(0, 0)
+        multiply_wq(0, 1)
+        multiply_wq(1, 0)
+        multiply_wq(1, 1)
+        multiply_wa(2)
+        multiply_wa(3)
+        round_xq(True, 0, 1, 0, HALF // 2)
+        round_xq(False, 0, 1, HALF // 2, HALF)
+        sigmoid(0)
+        sigmoid(1)
+        quantise_xq(0, 1)
+        round_xq(False, 1, 1, 0, HALF)
+        apply_gate(0)
+        quantise_xq(1, 1)
+        apply_gate(1)
+        multiply_wq(0, 2)
+        multiply_wq(0, 3)
+        multiply_wq(1, 2)
+        multiply_wq(1, 3)
+        round_wc(True, 0, 0, 0, P // 2)
+        sigmoid(2)
+        sigmoid(3)
+        round_wc(False, 0, 1, 0, P // 2)
+        quantise_wc(0, 0)
+        quantise_wc(0, 1)
+        apply_gate(2)
+        apply_gate(3)
+        for c in range(CHUNKS):
+            multiply_wc(0, c)
+        round_wc(True, 1, 0, 0, P // 2)
+        round_wc(True, 1, 1, 0, 20)
+        round_wc(False, 1, 1, 20, P // 2)
+        quantise_wc(1, 0)
+        quantise_wc(1, 1)
+        for c in range(CHUNKS):
+            multiply_wc(1, c)
+        for c in range(CHUNKS):
+            add_s(c)
+            round_y(c)
+            if c > 0:
+                quantise_y(c - 1)
+            if c == 2:
+                store_words(0, HALF)
+        quantise_y(CHUNKS - 1)
+        store_words(HALF, T)
+        for q in range(4):
+            queue = nc.scalar if q % 2 == 0 else nc.sync
+            queue.dma_start(
+                out=out_2[0, 4 * q : 4 * q + 4, :].bitcast(I32), in_=y_s[32 * q : 32 * q + 4, :].bitcast(I32)
+            )

@@ -19,10 +19,17 @@ P = 128
 PACK = 4
 PASSES = 2
 K_PASS = P * PACK
-CHUNK = 128
-CHUNKS = T // CHUNK
+QUADRANTS = 4
 HALF = T // 2
-PAD = 4
+PAIR = 2
+QUARTERS = [(h, u) for h in range(2) for u in range(2)]
+N_FP4 = 128
+LINE = 16
+GATE_PAD = 4
+
+XQ_SCALAR = (192, 160)
+WC_SCALAR = (40, 64)
+Y_SCALAR = 80
 
 
 def tile_mix_sum_and_its_own_gate_pl_kernel(
@@ -43,248 +50,231 @@ def tile_mix_sum_and_its_own_gate_pl_kernel(
         wq_sraw = tile("wq_sraw", [P, PASSES, N], U8)
         xt_w = tile("xt_w", [P, PASSES, 2 * T], U8)
         xt_s = tile("xt_s", [P, PASSES, T], U8)
+        xq_raw = [tile("xq_raw%d" % g, [P, PACK, T], F32) for g in range(PASSES)]
+        wc_raw = [tile("wc_raw%d" % g, [P, PACK, N], F32) for g in range(PASSES)]
         wa_w = tile("wa_w", [P, PACK, PASSES * P], U32)
         wa_s = tile("wa_s", [P, PACK, PASSES * P], U8)
         wq_w = tile("wq_w", [P, PACK, PASSES * 2 * P], U8)
         wq_s = tile("wq_s", [P, PACK, PASSES * P], U8)
-        pieces = [(z, h) for z in range(PASSES) for h in range(2)]
-        xq_raw = {zh: tile("xq_raw%d%d" % zh, [P, PACK, HALF], F32) for zh in pieces}
-        xq_bf = {zh: tile("xq_bf%d%d" % zh, [P, HALF, PACK], BF16) for zh in pieces}
-        xq_w = {zh: tile("xq_w%d%d" % zh, [P, HALF], U32) for zh in pieces}
-        xq_s = {zh: tile("xq_s%d%d" % zh, [P, HALF], U8) for zh in pieces}
-        wc_raw = {zh: tile("wc_raw%d%d" % zh, [P, PACK, HALF], F32) for zh in pieces}
-        wc_bf = {zh: tile("wc_bf%d%d" % zh, [P, PACK, P // 2, PACK], BF16) for zh in pieces}
-        zr = [(z, r) for z in range(PASSES) for r in range(PACK)]
-        wc_w = {k: tile("wc_w%d%d" % k, [P, P], U32) for k in zr}
-        wc_s = {k: tile("wc_s%d%d" % k, [P, P], U8) for k in zr}
+        wc_bf = [tile("wc_bf%d" % g, [P, PACK, P, PACK], BF16) for g in range(PASSES)]
+        wc_w = [tile("wc_w%d" % g, [P, PACK, P], U32) for g in range(PASSES)]
+        wc_s = [tile("wc_s%d" % g, [P, PACK, P], U8) for g in range(PASSES)]
+        xq_pieces = [(0, 0, T), (1, 0, HALF), (1, HALF, T)]
+        xq_bf = {k: tile("xq_bf%d_%d" % k[:2], [P, k[2] - k[1], PACK], BF16) for k in xq_pieces}
+        xq_w = {k: tile("xq_w%d_%d" % k[:2], [P, k[2] - k[1]], U32) for k in xq_pieces}
+        xq_s = {k: tile("xq_s%d_%d" % k[:2], [P, k[2] - k[1]], U8) for k in xq_pieces}
         zero = tile("zero", [P, PACK, 1], F32)
-        gate = tile("gate", [P, PACK, PAD + T], F32)
-        gated = [tile("gated%d" % c, [P, PACK, CHUNK], F32) for c in range(CHUNKS)]
-        y = [tile("y%d" % c, [P, PACK, CHUNK], F32) for c in range(CHUNKS)]
-        y_bf = [tile("y_bf%d" % c, [P, CHUNK, PACK], BF16) for c in range(CHUNKS)]
+        gate = tile("gate", [P, PACK, GATE_PAD + T], F32)
+        gated = {k: tile("gated%d%d" % k, [P, PAIR, HALF], F32) for k in QUARTERS}
+        y = [tile("y%d" % h, [P, PACK, HALF], F32) for h in range(2)]
+        y_bf = [tile("y_bf%d" % h, [P, HALF, PACK], BF16) for h in range(2)]
         y_w = tile("y_w", [P, T], U32)
         y_s = tile("y_s", [P, T], U8)
-        z_ps = [ps.tile([P, PACK, CHUNK], F32, name="z_ps%d" % c) for c in range(CHUNKS)]
-        s_ps = [ps.tile([P, PACK, CHUNK], F32, name="s_ps%d" % c) for c in range(CHUNKS)]
+        z_ps = {k: ps.tile([P, PAIR, HALF], F32, name="z_ps%d%d" % k) for k in QUARTERS}
+        s_ps = {k: ps.tile([P, PAIR, HALF], F32, name="s_ps%d%d" % k) for k in QUARTERS}
 
         def clear(engine, plane):
-            engine.memset(plane[:].rearrange("p z n -> p (z n)").bitcast(I32), 0)
+            engine.memset(plane[:].rearrange("p g n -> p (g n)").bitcast(I32), 0)
 
-        def load_scales(queue, plane, scales):
-            for q in range(4):
-                queue.dma_start(
+        def load_scales(plane, scales, quadrants):
+            for q in quadrants:
+                nc.sync.dma_start(
                     out=plane[32 * q : 32 * q + 4, :, :].bitcast(I32),
-                    in_=scales[:, 4 * q : 4 * q + 4, :].rearrange("z r n -> r z n").bitcast(I32),
+                    in_=scales[:, 4 * q : 4 * q + 4, :].rearrange("g i n -> i g n").bitcast(I32),
                 )
 
-        def load_rows(raw, src, z, h):
-            rows = src[z * K_PASS : (z + 1) * K_PASS, h * HALF : (h + 1) * HALF]
-            nc.sync.dma_start(out=raw[(z, h)][:], in_=rows.rearrange("(p j) c -> p j c", j=PACK))
+        def load_fp4(words, src):
+            nc.sync.dma_start(out=words[:].bitcast(I32), in_=src.rearrange("g p b -> p g b").bitcast(I32))
 
-        def copy(on_scalar, out, in_):
-            if on_scalar:
-                nc.scalar.copy(out=out, in_=in_)
-            else:
-                nc.vector.tensor_copy(out=out, in_=in_)
+        def load_pass(raw, src, g):
+            rows = src[g * K_PASS : (g + 1) * K_PASS, :]
+            nc.sync.dma_start(out=raw[g][:], in_=rows.rearrange("(p j) c -> p j c", j=PACK))
 
-        def round_xq(on_scalar, z, h, lo, hi):
-            copy(
-                on_scalar,
-                xq_bf[(z, h)][:, lo:hi, :].rearrange("p (c i) j -> p c j i", i=4),
-                xq_raw[(z, h)][:, :, lo:hi].rearrange("p j (c i) -> p c j i", i=4),
+        def deal_scales(plane, raw):
+            nc.vector.tensor_copy(
+                out=plane[:].rearrange("p r (b i) -> p b r i", i=LINE),
+                in_=raw[:].rearrange("p g (b i r) -> p (g b) r i", i=LINE, r=PACK),
             )
 
-        def quantise_xq(z, h):
+        def interleave(engine_copy, out, in_):
+            engine_copy(out=out.rearrange("p (c i) j -> p c j i", i=4), in_=in_.rearrange("p j (c i) -> p c j i", i=4))
+
+        def round_xq(piece):
+            g, lo, hi = piece
+            cut = XQ_SCALAR[g]
+            interleave(nc.scalar.copy, xq_bf[piece][:, :cut, :], xq_raw[g][:, :, lo : lo + cut])
+            interleave(nc.vector.tensor_copy, xq_bf[piece][:, cut:, :], xq_raw[g][:, :, lo + cut : hi])
+
+        def quantise_xq(piece):
             nc.vector.quantize_mx(
-                out=xq_w[(z, h)][:].bitcast(FP8X4),
-                scales=xq_s[(z, h)][:],
-                in_=xq_bf[(z, h)][:].rearrange("p c j -> p (c j)"),
+                out=xq_w[piece][:].bitcast(FP8X4),
+                scales=xq_s[piece][:],
+                in_=xq_bf[piece][:].rearrange("p c j -> p (c j)"),
             )
 
-        def round_wc(on_scalar, z, h, lo, hi):
-            copy(
-                on_scalar,
-                wc_bf[(z, h)][:, :, lo:hi, :].rearrange("p r m j -> p m r j"),
-                wc_raw[(z, h)][:, :, PACK * lo : PACK * hi].rearrange("p j (m r) -> p m r j", r=PACK),
-            )
+        def round_wc(g):
+            cut = WC_SCALAR[g]
+            for engine_copy, lo, hi in ((nc.vector.tensor_copy, cut, P), (nc.scalar.copy, 0, cut)):
+                engine_copy(
+                    out=wc_bf[g][:, :, lo:hi, :].rearrange("p r m j -> p m r j"),
+                    in_=wc_raw[g][:, :, PACK * lo : PACK * hi].rearrange("p j (m r) -> p m r j", r=PACK),
+                )
 
-        def quantise_wc(z, h):
-            cols = slice(h * P // 2, (h + 1) * P // 2)
-            for r in range(PACK):
+        def quantise_wc(g, r_step):
+            for r in range(0, PACK, r_step):
                 nc.vector.quantize_mx(
-                    out=wc_w[(z, r)][:, cols].bitcast(FP8X4),
-                    scales=wc_s[(z, r)][:, cols],
-                    in_=wc_bf[(z, h)][:, r, :, :].rearrange("p m j -> p (m j)"),
+                    out=wc_w[g][:, r : r + r_step, :].rearrange("p r m -> p (r m)").bitcast(FP8X4),
+                    scales=wc_s[g][:, r : r + r_step, :].rearrange("p r m -> p (r m)"),
+                    in_=wc_bf[g][:, r : r + r_step, :, :].rearrange("p r m j -> p (r m j)"),
                 )
 
-        def multiply_wa(c):
-            for z in range(PASSES):
-                for r in range(PACK):
-                    nc.tensor.matmul_mx(
-                        out=z_ps[c][:, r, :],
-                        lhsT=wa_w[:, r, z * P : (z + 1) * P].bitcast(FP8X4),
-                        lhsT_scale=wa_s[:, r, z * P : (z + 1) * P],
-                        rhs=xt_w[:, z, 2 * c * CHUNK : 2 * (c + 1) * CHUNK].bitcast(FP4X4),
-                        rhs_scale=xt_s[:, z, c * CHUNK : (c + 1) * CHUNK],
-                        start=(z == 0 and r == 0),
-                        stop=False,
-                    )
+        def xq_operand(g, lo, width):
+            piece = [k for k in xq_pieces if k[0] == g and k[1] <= lo < k[2]][0]
+            cols = slice(lo - piece[1], lo - piece[1] + width)
+            return xq_w[piece][:, cols].bitcast(FP8X4), xq_s[piece][:, cols]
 
-        def multiply_wq(z, c):
-            h, lo = divmod(c * CHUNK, HALF)
-            for r in range(PACK):
+        def multiply_wa(h, u):
+            for g in range(PASSES):
+                for r in range(PAIR * u, PAIR * (u + 1)):
+                    for lo in range(0, HALF, N_FP4):
+                        t0 = h * HALF + lo
+                        nc.tensor.matmul_mx(
+                            out=z_ps[(h, u)][:, r % PAIR, lo : lo + N_FP4],
+                            lhsT=wa_w[:, r, g * P : (g + 1) * P].bitcast(FP8X4),
+                            lhsT_scale=wa_s[:, r, g * P : (g + 1) * P],
+                            rhs=xt_w[:, g, 2 * t0 : 2 * (t0 + N_FP4)].bitcast(FP4X4),
+                            rhs_scale=xt_s[:, g, t0 : t0 + N_FP4],
+                            start=(g == 0 and r % PAIR == 0 and lo == 0),
+                            stop=False,
+                        )
+
+        def multiply_wq(h, u):
+            for g in range(PASSES):
+                for r in range(PAIR * u, PAIR * (u + 1)):
+                    for lo in range(0, HALF, N_FP4):
+                        rhs, rhs_scale = xq_operand(g, h * HALF + lo, N_FP4)
+                        nc.tensor.matmul_mx(
+                            out=z_ps[(h, u)][:, r % PAIR, lo : lo + N_FP4],
+                            lhsT=wq_w[:, r, 2 * g * P : 2 * (g + 1) * P].bitcast(FP4X4),
+                            lhsT_scale=wq_s[:, r, g * P : (g + 1) * P],
+                            rhs=rhs,
+                            rhs_scale=rhs_scale,
+                            start=False,
+                            stop=(g == PASSES - 1 and r % PAIR == PAIR - 1 and lo + N_FP4 == HALF),
+                        )
+
+        def multiply_wc(g, h, u):
+            rhs, rhs_scale = xq_operand(g, h * HALF, HALF)
+            for r in range(PAIR * u, PAIR * (u + 1)):
                 nc.tensor.matmul_mx(
-                    out=z_ps[c][:, r, :],
-                    lhsT=wq_w[:, r, 2 * z * P : 2 * (z + 1) * P].bitcast(FP4X4),
-                    lhsT_scale=wq_s[:, r, z * P : (z + 1) * P],
-                    rhs=xq_w[(z, h)][:, lo : lo + CHUNK].bitcast(FP8X4),
-                    rhs_scale=xq_s[(z, h)][:, lo : lo + CHUNK],
-                    start=False,
-                    stop=(z == PASSES - 1 and r == PACK - 1),
+                    out=s_ps[(h, u)][:, r % PAIR, :],
+                    lhsT=wc_w[g][:, r, :].bitcast(FP8X4),
+                    lhsT_scale=wc_s[g][:, r, :],
+                    rhs=rhs,
+                    rhs_scale=rhs_scale,
+                    start=(g == 0 and r % PAIR == 0),
+                    stop=(g == PASSES - 1 and r % PAIR == PAIR - 1),
                 )
 
-        def multiply_wc(z, c):
-            h, lo = divmod(c * CHUNK, HALF)
-            for r in range(PACK):
-                nc.tensor.matmul_mx(
-                    out=s_ps[c][:, r, :],
-                    lhsT=wc_w[(z, r)][:].bitcast(FP8X4),
-                    lhsT_scale=wc_s[(z, r)][:],
-                    rhs=xq_w[(z, h)][:, lo : lo + CHUNK].bitcast(FP8X4),
-                    rhs_scale=xq_s[(z, h)][:, lo : lo + CHUNK],
-                    start=(z == 0 and r == 0),
-                    stop=(z == PASSES - 1 and r == PACK - 1),
-                )
+        def sigmoid(h, u):
+            lo = GATE_PAD + h * HALF
+            width = min(HALF, T - 1 - h * HALF)
+            nc.scalar.activation(
+                out=gate[:, PAIR * u : PAIR * (u + 1), lo : lo + width], in_=z_ps[(h, u)][:, :, :width], func=ACT.Sigmoid
+            )
 
-        def sigmoid(c):
-            lo = PAD + c * CHUNK
-            nc.scalar.activation(out=gate[:, :, lo : lo + CHUNK], in_=z_ps[c][:], func=ACT.Sigmoid)
+        def apply_gate(h, u):
+            lo = GATE_PAD - 1 + h * HALF
+            nc.vector.tensor_tensor(
+                out=gated[(h, u)][:],
+                in0=z_ps[(h, u)][:],
+                in1=gate[:, PAIR * u : PAIR * (u + 1), lo : lo + HALF],
+                op=ALU.mult,
+            )
 
-        def apply_gate(c):
-            lo = PAD - 1 + c * CHUNK
-            nc.vector.tensor_tensor(out=gated[c][:], in0=z_ps[c][:], in1=gate[:, :, lo : lo + CHUNK], op=ALU.mult)
-
-        def add_s(c):
+        def add_s(h, u):
+            rows = y[h][:, PAIR * u : PAIR * (u + 1), :]
             nc.vector.scalar_tensor_tensor(
-                out=y[c][:].rearrange("p r t -> p (r t)"),
-                in0=s_ps[c][:].rearrange("p r t -> p (r t)"),
+                out=rows.rearrange("p r t -> p (r t)"),
+                in0=s_ps[(h, u)][:].rearrange("p r t -> p (r t)"),
                 scalar=0.5,
-                in1=gated[c][:].rearrange("p r t -> p (r t)"),
+                in1=gated[(h, u)][:].rearrange("p r t -> p (r t)"),
                 op0=ALU.mult,
                 op1=ALU.add,
             )
-            nc.sync.dma_start(
-                out=out_0[:, c * CHUNK : (c + 1) * CHUNK].rearrange("(p r) t -> p r t", r=PACK), in_=y[c][:]
-            )
+            dealt = out_0[:, h * HALF : (h + 1) * HALF].rearrange("(p r) t -> p r t", r=PACK)
+            nc.sync.dma_start(out=dealt[:, PAIR * u : PAIR * (u + 1), :], in_=rows)
 
-        def round_y(c):
-            nc.scalar.copy(
-                out=y_bf[c][:].rearrange("p (c i) r -> p c r i", i=4),
-                in_=y[c][:].rearrange("p r (c i) -> p c r i", i=4),
-            )
-
-        def quantise_y(c):
-            cols = slice(c * CHUNK, (c + 1) * CHUNK)
+        def quantise_y(h):
+            cols = slice(h * HALF, (h + 1) * HALF)
             nc.vector.quantize_mx(
-                out=y_w[:, cols].bitcast(FP8X4), scales=y_s[:, cols], in_=y_bf[c][:].rearrange("p t r -> p (t r)")
+                out=y_w[:, cols].bitcast(FP8X4), scales=y_s[:, cols], in_=y_bf[h][:].rearrange("p t r -> p (t r)")
             )
-
-        def store_words(lo, hi):
-            words = out_1[0].rearrange("p c r -> p (c r)").bitcast(I32)
-            nc.sync.dma_start(out=words[:, lo:hi], in_=y_w[:, lo:hi].bitcast(I32))
+            words = out_1[0].rearrange("p t r -> p (t r)").bitcast(I32)
+            nc.sync.dma_start(out=words[:, cols], in_=y_w[:, cols].bitcast(I32))
 
         clear(nc.vector, wa_sraw)
         clear(nc.gpsimd, xt_s)
         clear(nc.vector, wq_sraw)
         nc.vector.memset(zero[:], 0.0)
-        nc.scalar.activation(out=gate[:, :, PAD - 1 : PAD], in_=zero[:], func=ACT.Sigmoid)
-        load_scales(nc.gpsimd, xt_s, xt_scales)
+        nc.scalar.activation(out=gate[:, :, GATE_PAD - 1 : GATE_PAD], in_=zero[:], func=ACT.Sigmoid)
+
         nc.sync.dma_start(
-            out=wa_raw[:].rearrange("p (z n) -> p z n", z=PASSES).bitcast(I32),
-            in_=wa_words.rearrange("z p n t -> p z (n t)").bitcast(I32),
+            out=wa_raw[:].rearrange("p (g n) -> p g n", g=PASSES).bitcast(I32),
+            in_=wa_words.rearrange("g p n j -> p g (n j)").bitcast(I32),
         )
-        load_scales(nc.sync, wa_sraw, wa_scales)
-        nc.sync.dma_start(out=xt_w[:].bitcast(I32), in_=xt_words.rearrange("z p b -> p z b").bitcast(I32))
-        nc.sync.dma_start(out=wq_raw[:].bitcast(I32), in_=wq_words.rearrange("z p b -> p z b").bitcast(I32))
-        load_rows(xq_raw, xq, 0, 0)
-        load_scales(nc.sync, wq_sraw, wq_scales)
-        load_rows(xq_raw, xq, 1, 0)
-        load_rows(xq_raw, xq, 0, 1)
-        load_rows(xq_raw, xq, 1, 1)
-        for z, h in pieces:
-            load_rows(wc_raw, wc, z, h)
+        load_fp4(xt_w, xt_words)
+        load_fp4(wq_raw, wq_words)
+        load_scales(wa_sraw, wa_scales, range(QUADRANTS))
+        load_pass(xq_raw, xq, 0)
+        load_scales(xt_s, xt_scales, range(QUADRANTS))
+        load_scales(wq_sraw, wq_scales, range(QUADRANTS // 2))
+        load_pass(xq_raw, xq, 1)
+        load_scales(wq_sraw, wq_scales, range(QUADRANTS // 2, QUADRANTS))
+        for g in range(PASSES):
+            load_pass(wc_raw, wc, g)
 
         nc.vector.tensor_copy(
-            out=wa_w[:].bitcast(I32).rearrange("p r (b i) -> p b r i", i=4),
-            in_=wa_raw[:].bitcast(I32).rearrange("p (b i r) -> p b r i", i=4, r=PACK),
+            out=wa_w[:].bitcast(I32).rearrange("p r (b i) -> p b r i", i=LINE // 4),
+            in_=wa_raw[:].bitcast(I32).rearrange("p (b i r) -> p b r i", i=LINE // 4, r=PACK),
         )
-
-        def deal_scales(plane, raw):
-            nc.vector.tensor_copy(
-                out=plane[:].rearrange("p r (b i) -> p b r i", i=16),
-                in_=raw[:].rearrange("p z (b i r) -> p (z b) r i", i=16, r=PACK),
-            )
-
+        nc.vector.tensor_copy(
+            out=wq_w[:].rearrange("p r (b i e) -> p b r i e", i=LINE // 2, e=2),
+            in_=wq_raw[:].rearrange("p g (b i r e) -> p (g b) r i e", i=LINE // 2, r=PACK, e=2),
+        )
         deal_scales(wa_s, wa_sraw)
-        nc.vector.tensor_copy(
-            out=wq_w[:].rearrange("p r (b i u) -> p b r i u", i=8, u=2),
-            in_=wq_raw[:].rearrange("p z (b i r u) -> p (z b) r i u", i=8, r=PACK, u=2),
-        )
-        deal_scales(wq_s, wq_sraw)
+        for h, u in QUARTERS:
+            multiply_wa(h, u)
 
-        multiply_wa(0)
-        multiply_wa(1)
-        round_xq(True, 0, 0, 0, HALF)
-        round_xq(True, 1, 0, 0, HALF // 2)
-        round_xq(False, 1, 0, HALF // 2, HALF)
-        quantise_xq(0, 0)
-        quantise_xq(1, 0)
-        multiply_wq(0, 0)
-        multiply_wq(0, 1)
-        multiply_wq(1, 0)
-        multiply_wq(1, 1)
-        multiply_wa(2)
-        multiply_wa(3)
-        round_xq(True, 0, 1, 0, HALF // 2)
-        round_xq(False, 0, 1, HALF // 2, HALF)
-        sigmoid(0)
-        sigmoid(1)
-        quantise_xq(0, 1)
-        round_xq(False, 1, 1, 0, HALF)
-        apply_gate(0)
-        quantise_xq(1, 1)
-        apply_gate(1)
-        multiply_wq(0, 2)
-        multiply_wq(0, 3)
-        multiply_wq(1, 2)
-        multiply_wq(1, 3)
-        round_wc(True, 0, 0, 0, P // 2)
-        sigmoid(2)
-        sigmoid(3)
-        round_wc(False, 0, 1, 0, P // 2)
-        quantise_wc(0, 0)
-        quantise_wc(0, 1)
-        apply_gate(2)
-        apply_gate(3)
-        for c in range(CHUNKS):
-            multiply_wc(0, c)
-        round_wc(True, 1, 0, 0, P // 2)
-        round_wc(True, 1, 1, 0, 20)
-        round_wc(False, 1, 1, 20, P // 2)
-        quantise_wc(1, 0)
-        quantise_wc(1, 1)
-        for c in range(CHUNKS):
-            multiply_wc(1, c)
-        for c in range(CHUNKS):
-            add_s(c)
-            round_y(c)
-            if c > 0:
-                quantise_y(c - 1)
-            if c == 2:
-                store_words(0, HALF)
-        quantise_y(CHUNKS - 1)
-        store_words(HALF, T)
-        for q in range(4):
+        round_xq(xq_pieces[0])
+        quantise_xq(xq_pieces[0])
+        round_xq(xq_pieces[1])
+        deal_scales(wq_s, wq_sraw)
+        quantise_xq(xq_pieces[1])
+        round_xq(xq_pieces[2])
+        quantise_xq(xq_pieces[2])
+        for h, u in QUARTERS:
+            multiply_wq(h, u)
+
+        for g in range(PASSES):
+            sigmoid(g, 0)
+            round_wc(g)
+            apply_gate(g, 0)
+            quantise_wc(g, PACK if g < PASSES - 1 else 1)
+            sigmoid(g, 1)
+            apply_gate(g, 1)
+            for h, u in QUARTERS:
+                multiply_wc(g, h, u)
+
+        for h, u in QUARTERS:
+            add_s(h, u)
+            if (h, u) == (0, 1):
+                interleave(nc.scalar.copy, y_bf[0][:], y[0][:])
+        interleave(nc.scalar.copy, y_bf[1][:, :Y_SCALAR, :], y[1][:, :, :Y_SCALAR])
+        interleave(nc.vector.tensor_copy, y_bf[1][:, Y_SCALAR:, :], y[1][:, :, Y_SCALAR:])
+        quantise_y(0)
+        quantise_y(1)
+        for q in range(QUADRANTS):
             queue = nc.scalar if q % 2 == 0 else nc.sync
             queue.dma_start(
                 out=out_2[0, 4 * q : 4 * q + 4, :].bitcast(I32), in_=y_s[32 * q : 32 * q + 4, :].bitcast(I32)

@@ -23,13 +23,13 @@ QUADRANTS = 4
 HALF = T // 2
 PAIR = 2
 QUARTERS = [(h, u) for h in range(2) for u in range(2)]
+SHARED = (1, 0)
 N_FP4 = 128
 LINE = 16
 GATE_PAD = 4
 
 XQ_SCALAR = (192, 160)
-WC_SCALAR = (40, 64)
-Y_SCALAR = 80
+WC_SCALAR = (48, 64)
 
 
 def tile_mix_sum_and_its_own_gate_pl_kernel(
@@ -67,6 +67,7 @@ def tile_mix_sum_and_its_own_gate_pl_kernel(
         gate = tile("gate", [P, PACK, GATE_PAD + T], F32)
         gated = {k: tile("gated%d%d" % k, [P, PAIR, HALF], F32) for k in QUARTERS}
         y = [tile("y%d" % h, [P, PACK, HALF], F32) for h in range(2)]
+        half_s = tile("half_s", [P, PAIR, HALF], F32)
         y_bf = [tile("y_bf%d" % h, [P, HALF, PACK], BF16) for h in range(2)]
         y_w = tile("y_w", [P, T], U32)
         y_s = tile("y_s", [P, T], U8)
@@ -116,8 +117,8 @@ def tile_mix_sum_and_its_own_gate_pl_kernel(
             cut = WC_SCALAR[g]
             for engine_copy, lo, hi in ((nc.vector.tensor_copy, cut, P), (nc.scalar.copy, 0, cut)):
                 engine_copy(
-                    out=wc_bf[g][:, :, lo:hi, :].rearrange("p r m j -> p m r j"),
-                    in_=wc_raw[g][:, :, PACK * lo : PACK * hi].rearrange("p j (m r) -> p m r j", r=PACK),
+                    out=wc_bf[g][:, :, lo:hi, :].rearrange("p (u e) m j -> p u m j e", e=PAIR),
+                    in_=wc_raw[g][:, :, PACK * lo : PACK * hi].rearrange("p j (m u e) -> p u m j e", u=2, e=PAIR),
                 )
 
         def quantise_wc(g, r_step):
@@ -194,14 +195,21 @@ def tile_mix_sum_and_its_own_gate_pl_kernel(
 
         def add_s(h, u):
             rows = y[h][:, PAIR * u : PAIR * (u + 1), :]
-            nc.vector.scalar_tensor_tensor(
-                out=rows.rearrange("p r t -> p (r t)"),
-                in0=s_ps[(h, u)][:].rearrange("p r t -> p (r t)"),
-                scalar=0.5,
-                in1=gated[(h, u)][:].rearrange("p r t -> p (r t)"),
-                op0=ALU.mult,
-                op1=ALU.add,
-            )
+            if (h, u) == SHARED:
+                nc.scalar.activation(out=half_s[:], in_=s_ps[(h, u)][:], func=ACT.Copy, scale=0.5)
+                nc.gpsimd.tensor_tensor(out=rows, in0=half_s[:], in1=gated[(h, u)][:], op=ALU.add)
+            else:
+                nc.vector.scalar_tensor_tensor(
+                    out=rows.rearrange("p r t -> p (r t)"),
+                    in0=s_ps[(h, u)][:].rearrange("p r t -> p (r t)"),
+                    scalar=0.5,
+                    in1=gated[(h, u)][:].rearrange("p r t -> p (r t)"),
+                    op0=ALU.mult,
+                    op1=ALU.add,
+                )
+
+        def store_y(h, u):
+            rows = y[h][:, PAIR * u : PAIR * (u + 1), :]
             dealt = out_0[:, h * HALF : (h + 1) * HALF].rearrange("(p r) t -> p r t", r=PACK)
             nc.sync.dma_start(out=dealt[:, PAIR * u : PAIR * (u + 1), :], in_=rows)
 
@@ -238,11 +246,11 @@ def tile_mix_sum_and_its_own_gate_pl_kernel(
             out=wa_w[:].bitcast(I32).rearrange("p r (b i) -> p b r i", i=LINE // 4),
             in_=wa_raw[:].bitcast(I32).rearrange("p (b i r) -> p b r i", i=LINE // 4, r=PACK),
         )
+        deal_scales(wa_s, wa_sraw)
         nc.vector.tensor_copy(
             out=wq_w[:].rearrange("p r (b i e) -> p b r i e", i=LINE // 2, e=2),
             in_=wq_raw[:].rearrange("p g (b i r e) -> p (g b) r i e", i=LINE // 2, r=PACK, e=2),
         )
-        deal_scales(wa_s, wa_sraw)
         for h, u in QUARTERS:
             multiply_wa(h, u)
 
@@ -263,15 +271,18 @@ def tile_mix_sum_and_its_own_gate_pl_kernel(
             quantise_wc(g, PACK if g < PASSES - 1 else 1)
             sigmoid(g, 1)
             apply_gate(g, 1)
-            for h, u in QUARTERS:
+            for h, u in [SHARED] + [k for k in QUARTERS if k != SHARED]:
                 multiply_wc(g, h, u)
 
-        for h, u in QUARTERS:
-            add_s(h, u)
-            if (h, u) == (0, 1):
-                interleave(nc.scalar.copy, y_bf[0][:], y[0][:])
-        interleave(nc.scalar.copy, y_bf[1][:, :Y_SCALAR, :], y[1][:, :, :Y_SCALAR])
-        interleave(nc.vector.tensor_copy, y_bf[1][:, Y_SCALAR:, :], y[1][:, :, Y_SCALAR:])
+        add_s(*SHARED)
+        for u in range(2):
+            add_s(0, u)
+            store_y(0, u)
+        interleave(nc.scalar.copy, y_bf[0][:], y[0][:])
+        add_s(1, 1)
+        for u in range(2):
+            store_y(1, u)
+        interleave(nc.vector.tensor_copy, y_bf[1][:], y[1][:])
         quantise_y(0)
         quantise_y(1)
         for q in range(QUADRANTS):

from contextlib import ExitStack

import concourse.mybir as mybir

K, L, T, N = 1024, 1024, 512, 512
FLOPS = 2 * N * T * (K + 2 * L)

F32 = mybir.dt.float32
BF16 = mybir.dt.bfloat16
I32 = mybir.dt.int32
U32 = mybir.dt.uint32
U8 = mybir.dt.uint8
FP8X4 = mybir.dt.float8_e4m3fn_x4
FP4X4 = mybir.dt.float4_e2m1fn_x4
ALU = mybir.AluOpType
ACT = mybir.ActivationFunctionType

P = 128
PACK = 4
PASSES = 2
K_PASS = P * PACK
QUADRANTS = 4
HALF = T // 2
PAIR = 2
QUARTERS = [(h, u) for h in range(2) for u in range(2)]
SHARED = (1, 0)
N_FP4 = 128
LINE = 16
GATE_PAD = 4

XQ_SCALAR = (192, 160)
WC_SCALAR = (48, 64)


def tile_mix_sum_and_its_own_gate_pl_kernel(
    tc, xt_words, xt_scales, wa_words, wa_scales, xq, wq_words, wq_scales, wc, out_0, out_1, out_2
):
    nc = tc.nc
    with ExitStack() as ctx:
        sb = ctx.enter_context(tc.tile_pool(name="sb", bufs=1))
        ps = ctx.enter_context(tc.psum_pool(name="ps", bufs=1))
        ctx.enter_context(tc.manual_schedule())

        def tile(name, shape, dtype):
            return sb.tile(shape, dtype, name=name, align_bytes=64)

        wa_raw = tile("wa_raw", [P, PASSES * N], U32)
        wa_sraw = tile("wa_sraw", [P, PASSES, N], U8)
        wq_raw = tile("wq_raw", [P, PASSES, 2 * N], U8)
        wq_sraw = tile("wq_sraw", [P, PASSES, N], U8)
        xt_w = tile("xt_w", [P, PASSES, 2 * T], U8)
        xt_s = tile("xt_s", [P, PASSES, T], U8)
        xq_raw = [tile("xq_raw%d" % g, [P, PACK, T], F32) for g in range(PASSES)]
        wc_raw = [tile("wc_raw%d" % g, [P, PACK, N], F32) for g in range(PASSES)]
        wa_w = tile("wa_w", [P, PACK, PASSES * P], U32)
        wa_s = tile("wa_s", [P, PACK, PASSES * P], U8)
        wq_w = tile("wq_w", [P, PACK, PASSES * 2 * P], U8)
        wq_s = tile("wq_s", [P, PACK, PASSES * P], U8)
        wc_bf = [tile("wc_bf%d" % g, [P, PACK, P, PACK], BF16) for g in range(PASSES)]
        wc_w = [tile("wc_w%d" % g, [P, PACK, P], U32) for g in range(PASSES)]
        wc_s = [tile("wc_s%d" % g, [P, PACK, P], U8) for g in range(PASSES)]
        xq_pieces = [(0, 0, T), (1, 0, HALF), (1, HALF, T)]
        xq_bf = {k: tile("xq_bf%d_%d" % k[:2], [P, k[2] - k[1], PACK], BF16) for k in xq_pieces}
        xq_w = {k: tile("xq_w%d_%d" % k[:2], [P, k[2] - k[1]], U32) for k in xq_pieces}
        xq_s = {k: tile("xq_s%d_%d" % k[:2], [P, k[2] - k[1]], U8) for k in xq_pieces}
        zero = tile("zero", [P, PACK, 1], F32)
        gate = tile("gate", [P, PACK, GATE_PAD + T], F32)
        gated = {k: tile("gated%d%d" % k, [P, PAIR, HALF], F32) for k in QUARTERS}
        y = [tile("y%d" % h, [P, PACK, HALF], F32) for h in range(2)]
        half_s = tile("half_s", [P, PAIR, HALF], F32)
        y_bf = [tile("y_bf%d" % h, [P, HALF, PACK], BF16) for h in range(2)]
        y_w = tile("y_w", [P, T], U32)
        y_s = tile("y_s", [P, T], U8)
        z_ps = {k: ps.tile([P, PAIR, HALF], F32, name="z_ps%d%d" % k) for k in QUARTERS}
        s_ps = {k: ps.tile([P, PAIR, HALF], F32, name="s_ps%d%d" % k) for k in QUARTERS}

        def clear(engine, plane):
            engine.memset(plane[:].rearrange("p g n -> p (g n)").bitcast(I32), 0)

        def load_scales(plane, scales, quadrants):
            for q in quadrants:
                nc.sync.dma_start(
                    out=plane[32 * q : 32 * q + 4, :, :].bitcast(I32),
                    in_=scales[:, 4 * q : 4 * q + 4, :].rearrange("g i n -> i g n").bitcast(I32),
                )

        def load_fp4(words, src):
            nc.sync.dma_start(out=words[:].bitcast(I32), in_=src.rearrange("g p b -> p g b").bitcast(I32))

        def load_pass(raw, src, g):
            rows = src[g * K_PASS : (g + 1) * K_PASS, :]
            nc.sync.dma_start(out=raw[g][:], in_=rows.rearrange("(p j) c -> p j c", j=PACK))

        def deal_scales(plane, raw):
            nc.vector.tensor_copy(
                out=plane[:].rearrange("p r (b i) -> p b r i", i=LINE),
                in_=raw[:].rearrange("p g (b i r) -> p (g b) r i", i=LINE, r=PACK),
            )

        def interleave(engine_copy, out, in_):
            engine_copy(out=out.rearrange("p (c i) j -> p c j i", i=4), in_=in_.rearrange("p j (c i) -> p c j i", i=4))

        def round_xq(piece):
            g, lo, hi = piece
            cut = XQ_SCALAR[g]
            interleave(nc.scalar.copy, xq_bf[piece][:, :cut, :], xq_raw[g][:, :, lo : lo + cut])
            interleave(nc.vector.tensor_copy, xq_bf[piece][:, cut:, :], xq_raw[g][:, :, lo + cut : hi])

        def quantise_xq(piece):
            nc.vector.quantize_mx(
                out=xq_w[piece][:].bitcast(FP8X4),
                scales=xq_s[piece][:],
                in_=xq_bf[piece][:].rearrange("p c j -> p (c j)"),
            )

        def round_wc(g):
            cut = WC_SCALAR[g]
            for engine_copy, lo, hi in ((nc.vector.tensor_copy, cut, P), (nc.scalar.copy, 0, cut)):
                engine_copy(
                    out=wc_bf[g][:, :, lo:hi, :].rearrange("p (u e) m j -> p u m j e", e=PAIR),
                    in_=wc_raw[g][:, :, PACK * lo : PACK * hi].rearrange("p j (m u e) -> p u m j e", u=2, e=PAIR),
                )

        def quantise_wc(g, r_step):
            for r in range(0, PACK, r_step):
                nc.vector.quantize_mx(
                    out=wc_w[g][:, r : r + r_step, :].rearrange("p r m -> p (r m)").bitcast(FP8X4),
                    scales=wc_s[g][:, r : r + r_step, :].rearrange("p r m -> p (r m)"),
                    in_=wc_bf[g][:, r : r + r_step, :, :].rearrange("p r m j -> p (r m j)"),
                )

        def xq_operand(g, lo, width):
            piece = [k for k in xq_pieces if k[0] == g and k[1] <= lo < k[2]][0]
            cols = slice(lo - piece[1], lo - piece[1] + width)
            return xq_w[piece][:, cols].bitcast(FP8X4), xq_s[piece][:, cols]

        def multiply_wa(h, u):
            for g in range(PASSES):
                for r in range(PAIR * u, PAIR * (u + 1)):
                    for lo in range(0, HALF, N_FP4):
                        t0 = h * HALF + lo
                        nc.tensor.matmul_mx(
                            out=z_ps[(h, u)][:, r % PAIR, lo : lo + N_FP4],
                            lhsT=wa_w[:, r, g * P : (g + 1) * P].bitcast(FP8X4),
                            lhsT_scale=wa_s[:, r, g * P : (g + 1) * P],
                            rhs=xt_w[:, g, 2 * t0 : 2 * (t0 + N_FP4)].bitcast(FP4X4),
                            rhs_scale=xt_s[:, g, t0 : t0 + N_FP4],
                            start=(g == 0 and r % PAIR == 0 and lo == 0),
                            stop=False,
                        )

        def multiply_wq(h, u):
            for g in range(PASSES):
                for r in range(PAIR * u, PAIR * (u + 1)):
                    for lo in range(0, HALF, N_FP4):
                        rhs, rhs_scale = xq_operand(g, h * HALF + lo, N_FP4)
                        nc.tensor.matmul_mx(
                            out=z_ps[(h, u)][:, r % PAIR, lo : lo + N_FP4],
                            lhsT=wq_w[:, r, 2 * g * P : 2 * (g + 1) * P].bitcast(FP4X4),
                            lhsT_scale=wq_s[:, r, g * P : (g + 1) * P],
                            rhs=rhs,
                            rhs_scale=rhs_scale,
                            start=False,
                            stop=(g == PASSES - 1 and r % PAIR == PAIR - 1 and lo + N_FP4 == HALF),
                        )

        def multiply_wc(g, h, u):
            rhs, rhs_scale = xq_operand(g, h * HALF, HALF)
            for r in range(PAIR * u, PAIR * (u + 1)):
                nc.tensor.matmul_mx(
                    out=s_ps[(h, u)][:, r % PAIR, :],
                    lhsT=wc_w[g][:, r, :].bitcast(FP8X4),
                    lhsT_scale=wc_s[g][:, r, :],
                    rhs=rhs,
                    rhs_scale=rhs_scale,
                    start=(g == 0 and r % PAIR == 0),
                    stop=(g == PASSES - 1 and r % PAIR == PAIR - 1),
                )

        def sigmoid(h, u):
            lo = GATE_PAD + h * HALF
            width = min(HALF, T - 1 - h * HALF)
            nc.scalar.activation(
                out=gate[:, PAIR * u : PAIR * (u + 1), lo : lo + width], in_=z_ps[(h, u)][:, :, :width], func=ACT.Sigmoid
            )

        def apply_gate(h, u):
            lo = GATE_PAD - 1 + h * HALF
            nc.vector.tensor_tensor(
                out=gated[(h, u)][:],
                in0=z_ps[(h, u)][:],
                in1=gate[:, PAIR * u : PAIR * (u + 1), lo : lo + HALF],
                op=ALU.mult,
            )

        def add_s(h, u):
            rows = y[h][:, PAIR * u : PAIR * (u + 1), :]
            if (h, u) == SHARED:
                nc.scalar.activation(out=half_s[:], in_=s_ps[(h, u)][:], func=ACT.Copy, scale=0.5)
                nc.gpsimd.tensor_tensor(out=rows, in0=half_s[:], in1=gated[(h, u)][:], op=ALU.add)
            else:
                nc.vector.scalar_tensor_tensor(
                    out=rows.rearrange("p r t -> p (r t)"),
                    in0=s_ps[(h, u)][:].rearrange("p r t -> p (r t)"),
                    scalar=0.5,
                    in1=gated[(h, u)][:].rearrange("p r t -> p (r t)"),
                    op0=ALU.mult,
                    op1=ALU.add,
                )

        def store_y(h, u):
            rows = y[h][:, PAIR * u : PAIR * (u + 1), :]
            dealt = out_0[:, h * HALF : (h + 1) * HALF].rearrange("(p r) t -> p r t", r=PACK)
            nc.sync.dma_start(out=dealt[:, PAIR * u : PAIR * (u + 1), :], in_=rows)

        def quantise_y(h):
            cols = slice(h * HALF, (h + 1) * HALF)
            nc.vector.quantize_mx(
                out=y_w[:, cols].bitcast(FP8X4), scales=y_s[:, cols], in_=y_bf[h][:].rearrange("p t r -> p (t r)")
            )
            words = out_1[0].rearrange("p t r -> p (t r)").bitcast(I32)
            nc.sync.dma_start(out=words[:, cols], in_=y_w[:, cols].bitcast(I32))

        clear(nc.vector, wa_sraw)
        clear(nc.gpsimd, xt_s)
        clear(nc.vector, wq_sraw)
        nc.vector.memset(zero[:], 0.0)
        nc.scalar.activation(out=gate[:, :, GATE_PAD - 1 : GATE_PAD], in_=zero[:], func=ACT.Sigmoid)

        nc.sync.dma_start(
            out=wa_raw[:].rearrange("p (g n) -> p g n", g=PASSES).bitcast(I32),
            in_=wa_words.rearrange("g p n j -> p g (n j)").bitcast(I32),
        )
        load_fp4(xt_w, xt_words)
        load_fp4(wq_raw, wq_words)
        load_scales(wa_sraw, wa_scales, range(QUADRANTS))
        load_pass(xq_raw, xq, 0)
        load_scales(xt_s, xt_scales, range(QUADRANTS))
        load_scales(wq_sraw, wq_scales, range(QUADRANTS // 2))
        load_pass(xq_raw, xq, 1)
        load_scales(wq_sraw, wq_scales, range(QUADRANTS // 2, QUADRANTS))
        for g in range(PASSES):
            load_pass(wc_raw, wc, g)

        nc.vector.tensor_copy(
            out=wa_w[:].bitcast(I32).rearrange("p r (b i) -> p b r i", i=LINE // 4),
            in_=wa_raw[:].bitcast(I32).rearrange("p (b i r) -> p b r i", i=LINE // 4, r=PACK),
        )
        deal_scales(wa_s, wa_sraw)
        nc.vector.tensor_copy(
            out=wq_w[:].rearrange("p r (b i e) -> p b r i e", i=LINE // 2, e=2),
            in_=wq_raw[:].rearrange("p g (b i r e) -> p (g b) r i e", i=LINE // 2, r=PACK, e=2),
        )
        for h, u in QUARTERS:
            multiply_wa(h, u)

        round_xq(xq_pieces[0])
        quantise_xq(xq_pieces[0])
        round_xq(xq_pieces[1])
        deal_scales(wq_s, wq_sraw)
        quantise_xq(xq_pieces[1])
        round_xq(xq_pieces[2])
        quantise_xq(xq_pieces[2])
        for h, u in QUARTERS:
            multiply_wq(h, u)

        for g in range(PASSES):
            sigmoid(g, 0)
            round_wc(g)
            apply_gate(g, 0)
            quantise_wc(g, PACK if g < PASSES - 1 else 1)
            sigmoid(g, 1)
            apply_gate(g, 1)
            for h, u in [SHARED] + [k for k in QUARTERS if k != SHARED]:
                multiply_wc(g, h, u)

        add_s(*SHARED)
        for u in range(2):
            add_s(0, u)
            store_y(0, u)
        interleave(nc.scalar.copy, y_bf[0][:], y[0][:])
        add_s(1, 1)
        for u in range(2):
            store_y(1, u)
        interleave(nc.vector.tensor_copy, y_bf[1][:], y[1][:])
        quantise_y(0)
        quantise_y(1)
        for q in range(QUADRANTS):
            queue = nc.scalar if q % 2 == 0 else nc.sync
            queue.dma_start(
                out=out_2[0, 4 * q : 4 * q + 4, :].bitcast(I32), in_=y_s[32 * q : 32 * q + 4, :].bitcast(I32)
            )
